import numpy as np
import ml_dtypes


def mxq(x, axis, fmt="e4m3"):
    dtype, down = {"e4m3": (ml_dtypes.float8_e4m3fn, 7), "e5m2": (ml_dtypes.float8_e5m2, 14)}[fmt]
    v = np.moveaxis(np.asarray(x, np.float32).astype(ml_dtypes.bfloat16).astype(np.float64), axis, -1)
    blocks = v.reshape(v.shape[:-1] + (-1, 32))
    amax = np.abs(blocks).max(-1, keepdims=True)
    byte = np.maximum(np.where(amax > 0, np.frexp(amax)[1] - 1 + 127, 0) - down, 1)
    scale = np.exp2(byte - 127.0)
    codes = (blocks / scale).astype(np.float32).astype(dtype).astype(np.float64)
    return np.moveaxis((codes * scale).reshape(v.shape), -1, axis)


WIDE = False


def mx_kscale(k):
    if not WIDE:
        return np.ones(k)
    levels = np.array([10, -10, 5, -5, 0])
    if k % 512:
        return np.exp2(np.random.permutation(np.resize(levels, k // 32))).repeat(32)
    a = np.empty((k // 512, 16))
    for p in range(k // 512):
        a[p, :8] = np.random.permutation(np.resize(levels, 8))
        for g in range(8):
            far = levels[np.abs(levels - a[p, g]) >= 10]
            a[p, g + 8] = far[np.random.randint(len(far))]
    return np.exp2(a.ravel()).repeat(32)


def f64(x):
    return np.asarray(x).astype(np.float64)


def striped(idx):
    return np.tile(idx.reshape(-1, 16).T, (8, 1)).astype(np.uint16)


def unstriped(offs):
    return offs[:16].T.reshape(-1).astype(np.int64)


E2M1 = np.array([0.0, 0.5, 1.0, 1.5, 2.0, 3.0, 4.0, 6.0, -0.0, -0.5, -1.0, -1.5, -2.0, -3.0, -4.0, -6.0])


def pack_weight(w, fmt):
    k, n = w.shape
    w = f64(np.asarray(w, np.float32).astype(ml_dtypes.bfloat16)).reshape(k // 32, 32, n)
    amax = np.abs(w).max(1)
    if fmt == "e4m3":
        byte = np.frexp(amax)[1] - 1 + 127 - 7
    else:
        mant, ex = np.frexp(amax / 6.0)
        byte = np.where(mant > 0.5, ex, ex - 1) + 127
    byte = np.clip(np.where(amax > 0, byte, 1), 1, 254)
    scaled = (w * np.exp2(127.0 - byte)[:, None, :]).reshape(k, n).astype(np.float32)
    by_word = np.ascontiguousarray(scaled.reshape(k // 512, 128, 4, n).transpose(0, 1, 3, 2))
    if fmt == "e4m3":
        words = by_word.astype(ml_dtypes.float8_e4m3fn).view(np.uint8)
    else:
        c = by_word.astype(ml_dtypes.float4_e2m1fn).view(np.uint8) & 0xF
        words = (c[..., 0::2] | (c[..., 1::2] << 4)).reshape(k // 512, 128, 2 * n)
    return np.ascontiguousarray(words), np.ascontiguousarray(byte.astype(np.uint8).reshape(k // 512, 16, n))


def unpack_weight(words, scales, fmt):
    g, _, n = scales.shape
    words = np.ascontiguousarray(words).reshape(g, 128, n, -1)
    if fmt == "e4m3":
        vals = words.view(ml_dtypes.float8_e4m3fn).astype(np.float64)
    else:
        nib = np.empty((g, 128, n, 4), np.uint8)
        nib[..., 0::2] = words & 0xF
        nib[..., 1::2] = words >> 4
        vals = E2M1[nib]
    vals = vals * np.repeat(np.exp2(scales.astype(np.float64) - 127.0), 8, axis=1)[..., None]
    return vals.transpose(0, 1, 3, 2).reshape(g * 512, n)


def pack_table(v):
    words, scales = pack_weight(v, "e4m3")
    return np.concatenate([words.reshape(words.shape[0], -1), scales.reshape(scales.shape[0], -1)], axis=1)


def unpack_table(tab):
    g, t = tab.shape[0], tab.shape[1] // 528
    return unpack_weight(tab[:, :512 * t].reshape(g, 128, t, 4), tab[:, 512 * t:].reshape(g, 16, t), "e4m3")


def silu(v):
    return v / (1.0 + np.exp(-np.maximum(v, -700.0)))


K, L, M, T, S = 1024, 1536, 128, 2048, 1024


def setup_inputs():
    n = np.random.standard_normal
    s1 = mx_kscale(K)[:, None]
    s2 = mx_kscale(L)[:, None]
    p_w4 = pack_weight(n((K, M)) / np.sqrt(K) / s1, "e2m1")
    return {
        "tab": pack_table(n((K, T)) * s1),
        "w4_words": p_w4[0],
        "w4_scales": p_w4[1],
        "x": (n((L, S)) * s2).astype(np.float32),
        "u": (n((L, M)) / np.sqrt(L) / s2).astype(np.float32),
        "b": (0.3 * n(128)).astype(np.float32),
        "offs": striped(np.random.permutation(T)[:S]),
    }


def reference(tab, w4_words, w4_scales, x, u, b, offs):
    tab_ = unpack_table(tab)[:, unstriped(offs)]
    w4_ = unpack_weight(w4_words, w4_scales, "e2m1")
    x_ = mxq(f64(x), 0, "e4m3")
    u_ = mxq(f64(u), 0, "e4m3")
    y = tab_.T @ w4_ + x_.T @ u_
    return silu(y + f64(b)[None, :])

@@ -1,0 +1,193 @@
+from contextlib import ExitStack
+
+import concourse.mybir as mybir
+from concourse.masks import make_identity
+
+K, L, M, T, S = 1024, 1536, 128, 2048, 1024
+FLOPS = 2 * S * M * (K + L)
+
+F32 = mybir.dt.float32
+BF16 = mybir.dt.bfloat16
+I32 = mybir.dt.int32
+U32 = mybir.dt.uint32
+U16 = mybir.dt.uint16
+U8 = mybir.dt.uint8
+FP8X4 = mybir.dt.float8_e4m3fn_x4
+FP4X4 = mybir.dt.float4_e2m1fn_x4
+SILU = mybir.ActivationFunctionType.Silu
+ADD = mybir.AluOpType.add
+
+P = 128
+KP = 512
+A = K // KP
+G = L // KP
+NT = S // P
+
+
+def tile_list_tabx_tm_silu_kernel(tc, tab, w4_words, w4_scales, x, u, b, offs, out):
+    nc = tc.nc
+
+    with ExitStack() as ctx:
+        keep = ctx.enter_context(tc.tile_pool(name="keep", bufs=1))
+        psum = ctx.enter_context(tc.psum_pool(name="psum", bufs=1))
+
+        offsets = keep.tile([P, S // 16], U16, name="offsets")
+        u_raw = keep.tile([P, G, 4, M], F32, name="u_raw", align_bytes=64)
+        tab_sc = keep.tile([P, A, T // 4], I32, name="tab_sc", align_bytes=64)
+        words = [keep.tile([P, T], I32, name=f"words{a}", align_bytes=64) for a in range(A)]
+        w4_w = keep.tile([P, A, 2 * M], U8, name="w4_w", align_bytes=64)
+        w4_s = keep.tile([P, A, M // 4], I32, name="w4_s", align_bytes=64)
+        b_col = keep.tile([P, 1], F32, name="b_col", align_bytes=64)
+        ident = keep.tile([P, P], F32, name="ident", align_bytes=64)
+        warm = keep.tile([P, 1], F32, name="warm", align_bytes=64)
+        warm2 = keep.tile([P, 1], F32, name="warm2", align_bytes=64)
+
+        tab_i = tab.bitcast(I32)
+        nc.vector.memset(tab_sc[:], 0)
+        nc.vector.memset(w4_s[:], 0)
+        nc.vector.memset(warm[:], 0.0)
+        nc.sync.dma_start(offsets[:], offs)
+        nc.sync.dma_start(out=b_col[:], in_=b.rearrange("(p o) -> p o", o=1))
+        nc.sync.dma_start(out=w4_w[:].bitcast(I32), in_=w4_words.bitcast(I32).rearrange("a p n -> p a n"))
+        sc_i = tab_i[:, 128 * T : 132 * T].rearrange("a (q t) -> q a t", q=16)
+        def load_words(a):
+            nc.sync.dma_start(out=words[a][:], in_=tab_i[a, 0 : 128 * T].rearrange("(p t) -> p t", p=P))
+
+        x_raw = {}
+
+        def load_x(g, w0, w1):
+            t = keep.tile([P, 4, w1 - w0], F32, name=f"x_raw{g}_{w0}", align_bytes=64)
+            nc.sync.dma_start(out=t[:], in_=x[KP * g : KP * (g + 1), w0:w1].rearrange("(p j) w -> p j w", j=4))
+            x_raw[g, w0] = t
+
+        load_words(0)
+        for q in range(4):
+            nc.sync.dma_start(out=tab_sc[32 * q : 32 * q + 4], in_=sc_i[4 * q : 4 * q + 4])
+        nc.sync.dma_start(out=u_raw[:], in_=u.rearrange("(g p j) n -> p g j n", p=P, j=4))
+        w4s_i = w4_scales.bitcast(I32).rearrange("a q n -> q a n")
+        for q in range(4):
+            nc.sync.dma_start(out=w4_s[32 * q : 32 * q + 4], in_=w4s_i[4 * q : 4 * q + 4])
+        load_x(0, 0, S)
+        load_words(1)
+        load_x(1, 0, S)
+        load_x(2, 0, 512)
+        load_x(2, 512, 768)
+        load_x(2, 768, 1024)
+
+        make_identity(nc, ident[:])
+        nc.scalar.activation(warm2[:], warm[:], SILU)
+
+        def interleave(dst, src, w0, w1, by):
+            if w1 > w0:
+                o = dst[:, w0:w1, :].rearrange("p (c i) j -> p c j i", i=4)
+                s = src[:, :, w0:w1].rearrange("p j (c i) -> p c j i", i=4)
+                if by == "S":
+                    nc.scalar.copy(o, s)
+                else:
+                    nc.vector.tensor_copy(o, s)
+
+        u_bf = keep.tile([P, G, M, 4], BF16, name="u_bf", align_bytes=64)
+        u_c = keep.tile([P, G, M], U32, name="u_c", align_bytes=64)
+        u_s = keep.tile([P, G, M], U8, name="u_s", align_bytes=64)
+        for g in range(G):
+            interleave(u_bf[:, g], u_raw[:, g], 0, M, "S")
+        for g in range(G):
+            nc.vector.quantize_mx(
+                out=u_c[:, g].bitcast(FP8X4), scales=u_s[:, g], in_=u_bf[:, g].rearrange("p w j -> p (w j)")
+            )
+
+        gw = [keep.tile([P, S], U32, name=f"gw{a}", align_bytes=64) for a in range(A)]
+        gs = [keep.tile([P, S], U8, name=f"gs{a}", align_bytes=64) for a in range(A)]
+
+        def gather_scales(a):
+            nc.vector.tensor_copy(gs[a][:], tab_sc[:, a, :].bitcast(U8).indirect(offsets[:]))
+
+        def gather_words(a):
+            nc.vector.tensor_copy(gw[a][:], words[a][:].bitcast(U32).indirect(offsets[:]))
+
+        gather_scales(0)
+        gather_scales(1)
+        gather_words(0)
+
+        b_ps = psum.tile([P, 512], F32, name="b_ps", tag="bank7")
+        nc.tensor.transpose(b_ps[:, 0:M], b_col[:].to_broadcast([P, P]), ident[:])
+        b_all = keep.tile([P, M], F32, name="b_all", align_bytes=64)
+        nc.scalar.copy(b_all[:], b_ps[:, 0:M])
+
+        acc = [psum.tile([P, 512], F32, name=f"acc{t}", tag=f"bank{t}") for t in range(NT)]
+
+        def table_pass(a, t, start):
+            c = slice(P * t, P * (t + 1))
+            nc.tensor.matmul_mx(
+                out=acc[t][:, 0:M],
+                lhsT=gw[a][:, c].bitcast(FP8X4),
+                lhsT_scale=gs[a][:, c],
+                rhs=w4_w[:, a, :].bitcast(FP4X4),
+                rhs_scale=w4_s[:, a, :].bitcast(U8),
+                start=start,
+                stop=False,
+            )
+
+        for t in range(NT):
+            table_pass(0, t, True)
+
+        x_bf = [keep.tile([P, S, 4], BF16, name=f"x_bf{g}", align_bytes=64) for g in range(G)]
+        x_c = [keep.tile([P, S], U32, name=f"x_c{g}", align_bytes=64) for g in range(G)]
+        x_s = [keep.tile([P, S], U8, name=f"x_s{g}", align_bytes=64) for g in range(G)]
+
+        def x_group(g, load0, w0, w1, sc):
+            raw = x_raw[g, load0]
+            n = w1 - w0
+            dst = x_bf[g][:, w0:w1, :]
+            src = raw[:, :, w0 - load0 : w1 - load0]
+            interleave(dst, src, 0, sc, "S")
+            interleave(dst, src, sc, n, "V")
+            nc.vector.quantize_mx(
+                out=x_c[g][:, w0:w1].bitcast(FP8X4),
+                scales=x_s[g][:, w0:w1],
+                in_=dst.rearrange("p w j -> p (w j)"),
+            )
+
+        def x_pass(g, t):
+            c = slice(P * t, P * (t + 1))
+            nc.tensor.matmul_mx(
+                out=acc[t][:, 0:M],
+                lhsT=x_c[g][:, c].bitcast(FP8X4),
+                lhsT_scale=x_s[g][:, c],
+                rhs=u_c[:, g].bitcast(FP8X4),
+                rhs_scale=u_s[:, g],
+                start=False,
+                stop=(g == G - 1),
+            )
+
+        for w0 in (0, 512):
+            x_group(0, 0, w0, w0 + 512, 512)
+            for t in range(w0 // P, w0 // P + 4):
+                x_pass(0, t)
+
+        gather_words(1)
+        for t in range(NT):
+            table_pass(1, t, False)
+
+        for w0 in (0, 512):
+            x_group(1, 0, w0, w0 + 512, 384)
+            for t in range(w0 // P, w0 // P + 4):
+                x_pass(1, t)
+
+        y = keep.tile([P, NT, M], F32, name="y", align_bytes=64)
+        o = keep.tile([P, NT, M], F32, name="o", align_bytes=64)
+
+        def finish(t0, t1):
+            for t in range(t0, t1):
+                nc.vector.tensor_tensor(y[:, t], acc[t][:, 0:M], b_all[:], ADD)
+            nc.scalar.activation(o[:, t0:t1], y[:, t0:t1], SILU)
+            nc.sync.dma_start(
+                out=out[P * t0 : P * t1, :].rearrange("(t p) n -> p t n", p=P), in_=o[:, t0:t1]
+            )
+
+        for w0, w1, sc, step in ((0, 512, 320, 4), (512, 768, 144, 2), (768, 1024, 128, 1)):
+            x_group(2, w0, w0, w1, sc)
+            for t in range(w0 // P, w1 // P):
+                x_pass(2, t)
+            for t in range(w0 // P, w1 // P, step):
+                finish(t, t + step)

@@ -46,12 +46,14 @@ def tile_list_tabx_tm_silu_kernel(tc, tab, w4_words, w4_scales, x, u, b, offs, o
         nc.vector.memset(tab_sc[:], 0)
         nc.vector.memset(w4_s[:], 0)
         nc.vector.memset(warm[:], 0.0)
-        nc.sync.dma_start(offsets[:], offs)
-        nc.sync.dma_start(out=b_col[:], in_=b.rearrange("(p o) -> p o", o=1))
-        nc.sync.dma_start(out=w4_w[:].bitcast(I32), in_=w4_words.bitcast(I32).rearrange("a p n -> p a n"))
-        sc_i = tab_i[:, 128 * T : 132 * T].rearrange("a (q t) -> q a t", q=16)
+
         def load_words(a):
             nc.sync.dma_start(out=words[a][:], in_=tab_i[a, 0 : 128 * T].rearrange("(p t) -> p t", p=P))
+
+        def load_scales(tile, rows):
+            view = rows.rearrange("a (q r) n -> r q a n", r=4)
+            for r in range(4):
+                nc.sync.dma_start(out=tile[r:P:32], in_=view[r])
 
         x_raw = {}
 
@@ -61,17 +63,16 @@ def tile_list_tabx_tm_silu_kernel(tc, tab, w4_words, w4_scales, x, u, b, offs, o
             x_raw[g, w0] = t
 
         load_words(0)
-        for q in range(4):
-            nc.sync.dma_start(out=tab_sc[32 * q : 32 * q + 4], in_=sc_i[4 * q : 4 * q + 4])
+        nc.sync.dma_start(offsets[:], offs)
+        nc.sync.dma_start(out=b_col[:], in_=b.rearrange("(p o) -> p o", o=1))
+        load_scales(tab_sc, tab_i[:, 128 * T : 132 * T].rearrange("a (q t) -> a q t", q=16))
         nc.sync.dma_start(out=u_raw[:], in_=u.rearrange("(g p j) n -> p g j n", p=P, j=4))
-        w4s_i = w4_scales.bitcast(I32).rearrange("a q n -> q a n")
-        for q in range(4):
-            nc.sync.dma_start(out=w4_s[32 * q : 32 * q + 4], in_=w4s_i[4 * q : 4 * q + 4])
         load_x(0, 0, S)
+        nc.sync.dma_start(out=w4_w[:].bitcast(I32), in_=w4_words.bitcast(I32).rearrange("a p n -> p a n"))
+        load_scales(w4_s, w4_scales.bitcast(I32))
         load_words(1)
         load_x(1, 0, S)
-        load_x(2, 0, 512)
-        load_x(2, 512, 768)
+        load_x(2, 0, 768)
         load_x(2, 768, 1024)
 
         make_identity(nc, ident[:])
@@ -135,18 +136,22 @@ def tile_list_tabx_tm_silu_kernel(tc, tab, w4_words, w4_scales, x, u, b, offs, o
         x_c = [keep.tile([P, S], U32, name=f"x_c{g}", align_bytes=64) for g in range(G)]
         x_s = [keep.tile([P, S], U8, name=f"x_s{g}", align_bytes=64) for g in range(G)]
 
-        def x_group(g, load0, w0, w1, sc):
-            raw = x_raw[g, load0]
-            n = w1 - w0
+        def x_copy(g, load0, w0, w1, sc):
             dst = x_bf[g][:, w0:w1, :]
-            src = raw[:, :, w0 - load0 : w1 - load0]
+            src = x_raw[g, load0][:, :, w0 - load0 : w1 - load0]
             interleave(dst, src, 0, sc, "S")
-            interleave(dst, src, sc, n, "V")
+            interleave(dst, src, sc, w1 - w0, "V")
+
+        def x_quantize(g, w0, w1):
             nc.vector.quantize_mx(
                 out=x_c[g][:, w0:w1].bitcast(FP8X4),
                 scales=x_s[g][:, w0:w1],
-                in_=dst.rearrange("p w j -> p (w j)"),
+                in_=x_bf[g][:, w0:w1, :].rearrange("p w j -> p (w j)"),
             )
+
+        def x_group(g, load0, w0, w1, sc):
+            x_copy(g, load0, w0, w1, sc)
+            x_quantize(g, w0, w1)
 
         def x_pass(g, t):
             c = slice(P * t, P * (t + 1))
@@ -170,7 +175,7 @@ def tile_list_tabx_tm_silu_kernel(tc, tab, w4_words, w4_scales, x, u, b, offs, o
             table_pass(1, t, False)
 
         for w0 in (0, 512):
-            x_group(1, 0, w0, w0 + 512, 384)
+            x_group(1, 0, w0, w0 + 512, 336)
             for t in range(w0 // P, w0 // P + 4):
                 x_pass(1, t)
 
@@ -185,9 +190,18 @@ def tile_list_tabx_tm_silu_kernel(tc, tab, w4_words, w4_scales, x, u, b, offs, o
                 out=out[P * t0 : P * t1, :].rearrange("(t p) n -> p t n", p=P), in_=o[:, t0:t1]
             )
 
-        for w0, w1, sc, step in ((0, 512, 320, 4), (512, 768, 144, 2), (768, 1024, 128, 1)):
-            x_group(2, w0, w0, w1, sc)
-            for t in range(w0 // P, w1 // P):
-                x_pass(2, t)
-            for t in range(w0 // P, w1 // P, step):
-                finish(t, t + step)
+        x_copy(2, 0, 0, 512, 288)
+        x_copy(2, 0, 512, 768, 136)
+        x_quantize(2, 0, 512)
+        x_quantize(2, 512, 768)
+        for t in range(6):
+            x_pass(2, t)
+        finish(0, 4)
+        finish(4, 6)
+        x_copy(2, 768, 768, 896, 56)
+        x_copy(2, 768, 896, 1024, 56)
+        x_quantize(2, 768, 896)
+        x_quantize(2, 896, 1024)
+        for t in range(6, 8):
+            x_pass(2, t)
+            finish(t, t + 1)

@@ -37,6 +37,7 @@ def tile_list_tabx_tm_silu_kernel(tc, tab, w4_words, w4_scales, x, u, b, offs, o
         words = [keep.tile([P, T], I32, name=f"words{a}", align_bytes=64) for a in range(A)]
         w4_w = keep.tile([P, A, 2 * M], U8, name="w4_w", align_bytes=64)
         w4_s = keep.tile([P, A, M // 4], I32, name="w4_s", align_bytes=64)
+        b_row = keep.tile([P, M], F32, name="b_row", align_bytes=64)
         b_col = keep.tile([P, 1], F32, name="b_col", align_bytes=64)
         ident = keep.tile([P, P], F32, name="ident", align_bytes=64)
         warm = keep.tile([P, 1], F32, name="warm", align_bytes=64)
@@ -45,7 +46,8 @@ def tile_list_tabx_tm_silu_kernel(tc, tab, w4_words, w4_scales, x, u, b, offs, o
         tab_i = tab.bitcast(I32)
         nc.vector.memset(tab_sc[:], 0)
         nc.vector.memset(w4_s[:], 0)
-        nc.vector.memset(warm[:], 0.0)
+        nc.gpsimd.memset(warm[:], 0.0)
+        nc.gpsimd.memset(b_row[:], 0.0)
 
         def load_words(a):
             nc.sync.dma_start(out=words[a][:], in_=tab_i[a, 0 : 128 * T].rearrange("(p t) -> p t", p=P))
@@ -64,7 +66,7 @@ def tile_list_tabx_tm_silu_kernel(tc, tab, w4_words, w4_scales, x, u, b, offs, o
 
         load_words(0)
         nc.sync.dma_start(offsets[:], offs)
-        nc.sync.dma_start(out=b_col[:], in_=b.rearrange("(p o) -> p o", o=1))
+        nc.sync.dma_start(out=b_row[0:1, :], in_=b.rearrange("(o n) -> o n", o=1))
         load_scales(tab_sc, tab_i[:, 128 * T : 132 * T].rearrange("a (q t) -> a q t", q=16))
         nc.sync.dma_start(out=u_raw[:], in_=u.rearrange("(g p j) n -> p g j n", p=P, j=4))
         load_x(0, 0, S)
@@ -111,9 +113,11 @@ def tile_list_tabx_tm_silu_kernel(tc, tab, w4_words, w4_scales, x, u, b, offs, o
         gather_words(0)
 
         b_ps = psum.tile([P, 512], F32, name="b_ps", tag="bank7")
-        nc.tensor.transpose(b_ps[:, 0:M], b_col[:].to_broadcast([P, P]), ident[:])
+        nc.tensor.transpose(b_ps[:, 0:P], b_row[:], ident[:])
+        nc.scalar.copy(b_col[:], b_ps[:, 0:1])
+        nc.tensor.transpose(b_ps[:, P : P + M], b_col[:].to_broadcast([P, P]), ident[:])
         b_all = keep.tile([P, M], F32, name="b_all", align_bytes=64)
-        nc.scalar.copy(b_all[:], b_ps[:, 0:M])
+        nc.scalar.copy(b_all[:], b_ps[:, P : P + M])
 
         acc = [psum.tile([P, 512], F32, name=f"acc{t}", tag=f"bank{t}") for t in range(NT)]
 
@@ -175,7 +179,7 @@ def tile_list_tabx_tm_silu_kernel(tc, tab, w4_words, w4_scales, x, u, b, offs, o
             table_pass(1, t, False)
 
         for w0 in (0, 512):
-            x_group(1, 0, w0, w0 + 512, 336)
+            x_group(1, 0, w0, w0 + 512, 272)
             for t in range(w0 // P, w0 // P + 4):
                 x_pass(1, t)
 
@@ -190,18 +194,15 @@ def tile_list_tabx_tm_silu_kernel(tc, tab, w4_words, w4_scales, x, u, b, offs, o
                 out=out[P * t0 : P * t1, :].rearrange("(t p) n -> p t n", p=P), in_=o[:, t0:t1]
             )
 
-        x_copy(2, 0, 0, 512, 288)
-        x_copy(2, 0, 512, 768, 136)
-        x_quantize(2, 0, 512)
-        x_quantize(2, 512, 768)
-        for t in range(6):
-            x_pass(2, t)
-        finish(0, 4)
-        finish(4, 6)
-        x_copy(2, 768, 768, 896, 56)
-        x_copy(2, 768, 896, 1024, 56)
-        x_quantize(2, 768, 896)
-        x_quantize(2, 896, 1024)
+        for w0 in (0, 256, 512):
+            x_copy(2, 0, w0, w0 + 256, 136)
+        for w0 in (0, 256, 512):
+            x_quantize(2, w0, w0 + 256)
+            for t in (w0 // P, w0 // P + 1):
+                x_pass(2, t)
+        for t in (0, 2, 4):
+            finish(t, t + 2)
+        x_group(2, 768, 768, 1024, 104)
         for t in range(6, 8):
             x_pass(2, t)
             finish(t, t + 1)

@@ -200,9 +200,13 @@ def tile_list_tabx_tm_silu_kernel(tc, tab, w4_words, w4_scales, x, u, b, offs, o
             x_quantize(2, w0, w0 + 256)
             for t in (w0 // P, w0 // P + 1):
                 x_pass(2, t)
-        for t in (0, 2, 4):
+        for t in (0, 2):
             finish(t, t + 2)
-        x_group(2, 768, 768, 1024, 104)
+        x_copy(2, 768, 768, 896, 64)
+        x_copy(2, 768, 896, 1024, 64)
+        finish(4, 6)
+        x_quantize(2, 768, 896)
+        x_quantize(2, 896, 1024)
         for t in range(6, 8):
             x_pass(2, t)
             finish(t, t + 1)

from contextlib import ExitStack

import concourse.mybir as mybir
from concourse.masks import make_identity

K, L, M, T, S = 1024, 1536, 128, 2048, 1024
FLOPS = 2 * S * M * (K + L)

F32 = mybir.dt.float32
BF16 = mybir.dt.bfloat16
I32 = mybir.dt.int32
U32 = mybir.dt.uint32
U16 = mybir.dt.uint16
U8 = mybir.dt.uint8
FP8X4 = mybir.dt.float8_e4m3fn_x4
FP4X4 = mybir.dt.float4_e2m1fn_x4
SILU = mybir.ActivationFunctionType.Silu
ADD = mybir.AluOpType.add

P = 128
KP = 512
A = K // KP
G = L // KP
NT = S // P


def tile_list_tabx_tm_silu_kernel(tc, tab, w4_words, w4_scales, x, u, b, offs, out):
    nc = tc.nc

    with ExitStack() as ctx:
        keep = ctx.enter_context(tc.tile_pool(name="keep", bufs=1))
        psum = ctx.enter_context(tc.psum_pool(name="psum", bufs=1))

        offsets = keep.tile([P, S // 16], U16, name="offsets")
        u_raw = keep.tile([P, G, 4, M], F32, name="u_raw", align_bytes=64)
        tab_sc = keep.tile([P, A, T // 4], I32, name="tab_sc", align_bytes=64)
        words = [keep.tile([P, T], I32, name=f"words{a}", align_bytes=64) for a in range(A)]
        w4_w = keep.tile([P, A, 2 * M], U8, name="w4_w", align_bytes=64)
        w4_s = keep.tile([P, A, M // 4], I32, name="w4_s", align_bytes=64)
        b_row = keep.tile([P, M], F32, name="b_row", align_bytes=64)
        b_col = keep.tile([P, 1], F32, name="b_col", align_bytes=64)
        ident = keep.tile([P, P], F32, name="ident", align_bytes=64)
        warm = keep.tile([P, 1], F32, name="warm", align_bytes=64)
        warm2 = keep.tile([P, 1], F32, name="warm2", align_bytes=64)

        tab_i = tab.bitcast(I32)
        nc.vector.memset(tab_sc[:], 0)
        nc.vector.memset(w4_s[:], 0)
        nc.gpsimd.memset(warm[:], 0.0)
        nc.gpsimd.memset(b_row[:], 0.0)

        def load_words(a):
            nc.sync.dma_start(out=words[a][:], in_=tab_i[a, 0 : 128 * T].rearrange("(p t) -> p t", p=P))

        def load_scales(tile, rows):
            view = rows.rearrange("a (q r) n -> r q a n", r=4)
            for r in range(4):
                nc.sync.dma_start(out=tile[r:P:32], in_=view[r])

        x_raw = {}

        def load_x(g, w0, w1):
            t = keep.tile([P, 4, w1 - w0], F32, name=f"x_raw{g}_{w0}", align_bytes=64)
            nc.sync.dma_start(out=t[:], in_=x[KP * g : KP * (g + 1), w0:w1].rearrange("(p j) w -> p j w", j=4))
            x_raw[g, w0] = t

        load_words(0)
        nc.sync.dma_start(offsets[:], offs)
        nc.sync.dma_start(out=b_row[0:1, :], in_=b.rearrange("(o n) -> o n", o=1))
        load_scales(tab_sc, tab_i[:, 128 * T : 132 * T].rearrange("a (q t) -> a q t", q=16))
        nc.sync.dma_start(out=u_raw[:], in_=u.rearrange("(g p j) n -> p g j n", p=P, j=4))
        load_x(0, 0, S)
        nc.sync.dma_start(out=w4_w[:].bitcast(I32), in_=w4_words.bitcast(I32).rearrange("a p n -> p a n"))
        load_scales(w4_s, w4_scales.bitcast(I32))
        load_words(1)
        load_x(1, 0, S)
        load_x(2, 0, 768)
        load_x(2, 768, 1024)

        make_identity(nc, ident[:])
        nc.scalar.activation(warm2[:], warm[:], SILU)

        def interleave(dst, src, w0, w1, by):
            if w1 > w0:
                o = dst[:, w0:w1, :].rearrange("p (c i) j -> p c j i", i=4)
                s = src[:, :, w0:w1].rearrange("p j (c i) -> p c j i", i=4)
                if by == "S":
                    nc.scalar.copy(o, s)
                else:
                    nc.vector.tensor_copy(o, s)

        u_bf = keep.tile([P, G, M, 4], BF16, name="u_bf", align_bytes=64)
        u_c = keep.tile([P, G, M], U32, name="u_c", align_bytes=64)
        u_s = keep.tile([P, G, M], U8, name="u_s", align_bytes=64)
        for g in range(G):
            interleave(u_bf[:, g], u_raw[:, g], 0, M, "S")
        for g in range(G):
            nc.vector.quantize_mx(
                out=u_c[:, g].bitcast(FP8X4), scales=u_s[:, g], in_=u_bf[:, g].rearrange("p w j -> p (w j)")
            )

        gw = [keep.tile([P, S], U32, name=f"gw{a}", align_bytes=64) for a in range(A)]
        gs = [keep.tile([P, S], U8, name=f"gs{a}", align_bytes=64) for a in range(A)]

        def gather_scales(a):
            nc.vector.tensor_copy(gs[a][:], tab_sc[:, a, :].bitcast(U8).indirect(offsets[:]))

        def gather_words(a):
            nc.vector.tensor_copy(gw[a][:], words[a][:].bitcast(U32).indirect(offsets[:]))

        gather_scales(0)
        gather_scales(1)
        gather_words(0)

        b_ps = psum.tile([P, 512], F32, name="b_ps", tag="bank7")
        nc.tensor.transpose(b_ps[:, 0:P], b_row[:], ident[:])
        nc.scalar.copy(b_col[:], b_ps[:, 0:1])
        nc.tensor.transpose(b_ps[:, P : P + M], b_col[:].to_broadcast([P, P]), ident[:])
        b_all = keep.tile([P, M], F32, name="b_all", align_bytes=64)
        nc.scalar.copy(b_all[:], b_ps[:, P : P + M])

        acc = [psum.tile([P, 512], F32, name=f"acc{t}", tag=f"bank{t}") for t in range(NT)]

        def table_pass(a, t, start):
            c = slice(P * t, P * (t + 1))
            nc.tensor.matmul_mx(
                out=acc[t][:, 0:M],
                lhsT=gw[a][:, c].bitcast(FP8X4),
                lhsT_scale=gs[a][:, c],
                rhs=w4_w[:, a, :].bitcast(FP4X4),
                rhs_scale=w4_s[:, a, :].bitcast(U8),
                start=start,
                stop=False,
            )

        for t in range(NT):
            table_pass(0, t, True)

        x_bf = [keep.tile([P, S, 4], BF16, name=f"x_bf{g}", align_bytes=64) for g in range(G)]
        x_c = [keep.tile([P, S], U32, name=f"x_c{g}", align_bytes=64) for g in range(G)]
        x_s = [keep.tile([P, S], U8, name=f"x_s{g}", align_bytes=64) for g in range(G)]

        def x_copy(g, load0, w0, w1, sc):
            dst = x_bf[g][:, w0:w1, :]
            src = x_raw[g, load0][:, :, w0 - load0 : w1 - load0]
            interleave(dst, src, 0, sc, "S")
            interleave(dst, src, sc, w1 - w0, "V")

        def x_quantize(g, w0, w1):
            nc.vector.quantize_mx(
                out=x_c[g][:, w0:w1].bitcast(FP8X4),
                scales=x_s[g][:, w0:w1],
                in_=x_bf[g][:, w0:w1, :].rearrange("p w j -> p (w j)"),
            )

        def x_group(g, load0, w0, w1, sc):
            x_copy(g, load0, w0, w1, sc)
            x_quantize(g, w0, w1)

        def x_pass(g, t):
            c = slice(P * t, P * (t + 1))
            nc.tensor.matmul_mx(
                out=acc[t][:, 0:M],
                lhsT=x_c[g][:, c].bitcast(FP8X4),
                lhsT_scale=x_s[g][:, c],
                rhs=u_c[:, g].bitcast(FP8X4),
                rhs_scale=u_s[:, g],
                start=False,
                stop=(g == G - 1),
            )

        for w0 in (0, 512):
            x_group(0, 0, w0, w0 + 512, 512)
            for t in range(w0 // P, w0 // P + 4):
                x_pass(0, t)

        gather_words(1)
        for t in range(NT):
            table_pass(1, t, False)

        for w0 in (0, 512):
            x_group(1, 0, w0, w0 + 512, 272)
            for t in range(w0 // P, w0 // P + 4):
                x_pass(1, t)

        y = keep.tile([P, NT, M], F32, name="y", align_bytes=64)
        o = keep.tile([P, NT, M], F32, name="o", align_bytes=64)

        def finish(t0, t1):
            for t in range(t0, t1):
                nc.vector.tensor_tensor(y[:, t], acc[t][:, 0:M], b_all[:], ADD)
            nc.scalar.activation(o[:, t0:t1], y[:, t0:t1], SILU)
            nc.sync.dma_start(
                out=out[P * t0 : P * t1, :].rearrange("(t p) n -> p t n", p=P), in_=o[:, t0:t1]
            )

        for w0 in (0, 256, 512):
            x_copy(2, 0, w0, w0 + 256, 136)
        for w0 in (0, 256, 512):
            x_quantize(2, w0, w0 + 256)
            for t in (w0 // P, w0 // P + 1):
                x_pass(2, t)
        for t in (0, 2):
            finish(t, t + 2)
        x_copy(2, 768, 768, 896, 64)
        x_copy(2, 768, 896, 1024, 64)
        finish(4, 6)
        x_quantize(2, 768, 896)
        x_quantize(2, 896, 1024)
        for t in range(6, 8):
            x_pass(2, t)
            finish(t, t + 1)
